import numpy as np
import ml_dtypes


def mxq(x, axis, fmt="e4m3"):
    dtype, down = {"e4m3": (ml_dtypes.float8_e4m3fn, 7), "e5m2": (ml_dtypes.float8_e5m2, 14)}[fmt]
    v = np.moveaxis(np.asarray(x, np.float32).astype(ml_dtypes.bfloat16).astype(np.float64), axis, -1)
    blocks = v.reshape(v.shape[:-1] + (-1, 32))
    amax = np.abs(blocks).max(-1, keepdims=True)
    byte = np.maximum(np.where(amax > 0, np.frexp(amax)[1] - 1 + 127, 0) - down, 1)
    scale = np.exp2(byte - 127.0)
    codes = (blocks / scale).astype(np.float32).astype(dtype).astype(np.float64)
    return np.moveaxis((codes * scale).reshape(v.shape), -1, axis)


WIDE = False


def mx_kscale(k):
    if not WIDE:
        return np.ones(k)
    levels = np.array([10, -10, 5, -5, 0])
    if k % 512:
        return np.exp2(np.random.permutation(np.resize(levels, k // 32))).repeat(32)
    a = np.empty((k // 512, 16))
    for p in range(k // 512):
        a[p, :8] = np.random.permutation(np.resize(levels, 8))
        for g in range(8):
            far = levels[np.abs(levels - a[p, g]) >= 10]
            a[p, g + 8] = far[np.random.randint(len(far))]
    return np.exp2(a.ravel()).repeat(32)


def f64(x):
    return np.asarray(x).astype(np.float64)


def striped(idx):
    return np.tile(np.asarray(idx).reshape(-1, 16).T, (8, 1)).astype(np.uint16)


def unstriped(offs):
    return offs[:16].T.reshape(-1).astype(np.int64)


E2M1 = np.array([0.0, 0.5, 1.0, 1.5, 2.0, 3.0, 4.0, 6.0, -0.0, -0.5, -1.0, -1.5, -2.0, -3.0, -4.0, -6.0])


def pack_weight(w, fmt):
    k, n = w.shape
    w = f64(np.asarray(w, np.float32).astype(ml_dtypes.bfloat16)).reshape(k // 32, 32, n)
    amax = np.abs(w).max(1)
    if fmt == "e4m3":
        byte = np.frexp(amax)[1] - 1 + 127 - 7
    else:
        mant, ex = np.frexp(amax / 6.0)
        byte = np.where(mant > 0.5, ex, ex - 1) + 127
    byte = np.clip(np.where(amax > 0, byte, 1), 1, 254)
    scaled = (w * np.exp2(127.0 - byte)[:, None, :]).reshape(k, n).astype(np.float32)
    by_word = np.ascontiguousarray(scaled.reshape(k // 512, 128, 4, n).transpose(0, 1, 3, 2))
    if fmt == "e4m3":
        words = by_word.astype(ml_dtypes.float8_e4m3fn).view(np.uint8)
    else:
        c = by_word.astype(ml_dtypes.float4_e2m1fn).view(np.uint8) & 0xF
        words = (c[..., 0::2] | (c[..., 1::2] << 4)).reshape(k // 512, 128, 2 * n)
    return np.ascontiguousarray(words), np.ascontiguousarray(byte.astype(np.uint8).reshape(k // 512, 16, n))


def unpack_weight(words, scales, fmt):
    g, _, n = scales.shape
    words = np.ascontiguousarray(words).reshape(g, 128, n, -1)
    if fmt == "e4m3":
        vals = words.view(ml_dtypes.float8_e4m3fn).astype(np.float64)
    else:
        nib = np.empty((g, 128, n, 4), np.uint8)
        nib[..., 0::2] = words & 0xF
        nib[..., 1::2] = words >> 4
        vals = E2M1[nib]
    vals = vals * np.repeat(np.exp2(scales.astype(np.float64) - 127.0), 8, axis=1)[..., None]
    return vals.transpose(0, 1, 3, 2).reshape(g * 512, n)


K, R, F, T, J, G = 512, 128, 512, 2048, 512, 64


def setup_inputs():
    n = np.random.standard_normal
    idx = np.random.permutation(T)[:J]
    fk = mx_kscale(K)
    ff = mx_kscale(F)
    fj = mx_kscale(J)
    tj = np.ones(T)
    tj[idx] = fj
    tabp = pack_weight(n((K, T)) / fk[:, None], "e2m1")
    return {
        "tab_words": tabp[0],
        "tab_scales": tabp[1],
        "w1": (n((K, R)) * 1 / np.sqrt(K) * fk[:, None]).astype(np.float32),
        "share": (np.random.uniform(0.3, 1.2, (R, 1))).astype(np.float32),
        "wo": (n((F, R)) * 1 / np.sqrt(F) * ff[:, None]).astype(np.float32),
        "dy": (n((F, G)) / ff[:, None]).astype(np.float32),
        "js": (np.random.uniform(0.5, 2.0, (1, J)) * fj).astype(np.float32),
        "xrows": (n((K, T)) / tj).astype(np.float32),
        "old": (n((K, R)) * 4.0).astype(np.float32),
        "offs": striped(idx),
    }


def reference(tab_words, tab_scales, w1, share, wo, dy, js, xrows, old, offs):
    idx = unstriped(offs)
    tabu = unpack_weight(tab_words, tab_scales, "e2m1")
    w1q = mxq(f64(w1), 0, "e4m3")
    tabidxg = tabu[:, idx]
    a = w1q.T @ tabidxg
    m1 = a.reshape(R, G, J // G).mean(axis=2)
    v1 = np.sqrt(np.square(a).reshape(R, G, J // G).mean(axis=2) - np.square(m1) + 0.05)
    u1 = np.tanh(v1 + m1 * f64(share))
    woq = mxq(f64(wo), 0, "e4m3")
    dyq = mxq(f64(dy), 0, "e4m3")
    c0 = woq.T @ dyq
    dv1 = c0 * (1.0 - np.square(u1))
    e1 = dv1 * 0.5 / np.sqrt(np.square(a).reshape(R, G, J // G).mean(axis=2) - np.square(m1) + 0.05) / 8.0
    r1 = np.repeat(e1, J // G, axis=1)
    dm1 = c0 * (1.0 - np.square(u1)) * f64(share) + dv1 * 0.5 / np.sqrt(np.square(a).reshape(R, G, J // G).mean(axis=2) - np.square(m1) + 0.05) * (-1.0) * m1 * 2.0
    e2 = dm1 / 8.0
    r2 = np.repeat(e2, J // G, axis=1)
    da = r1 * a * 2.0 + r2
    gs = da * f64(js)
    gt1 = gs.T
    xt = f64(xrows)[:, idx].T
    xtq = mxq(xt, 0, "e4m3")
    gt1q = mxq(gt1, 0, "e4m3")
    gw = xtq.T @ gt1q
    y = gw + f64(old)
    return y

@@ -1,0 +1,187 @@
+from contextlib import ExitStack
+
+import concourse.mybir as mybir
+from concourse.masks import make_identity
+
+K, R, F, T, J, G = 512, 128, 512, 2048, 512, 64
+GROUP = J // G
+EPS = 0.05
+P = 128
+PACK = 4
+HALF = J // 2
+FLOPS = 2 * K * R * J + 2 * F * R * G + 2 * J * K * R
+
+F32 = mybir.dt.float32
+BF16 = mybir.dt.bfloat16
+I32 = mybir.dt.int32
+U32 = mybir.dt.uint32
+U16 = mybir.dt.uint16
+U8 = mybir.dt.uint8
+FP8X4 = mybir.dt.float8_e4m3fn_x4
+FP4X4 = mybir.dt.float4_e2m1fn_x4
+ALU = mybir.AluOpType
+ACT = mybir.ActivationFunctionType
+AX = mybir.AxisListType
+
+
+def tile_attend_cspreadpool_w_kernel(tc, tab_words, tab_scales, w1, share, wo, dy, js, xrows, old, offs, out):
+    nc = tc.nc
+    with ExitStack() as ctx:
+        sb = ctx.enter_context(tc.tile_pool(name="sb", bufs=1))
+        ps = ctx.enter_context(tc.psum_pool(name="ps", bufs=1))
+        ps2 = ctx.enter_context(tc.psum_pool(name="ps2", bufs=2))
+
+        def quantise(name, grouped, width, after=None, codes=None):
+            if codes is None:
+                codes = sb.tile([P, width], U32, name=name + "_codes", tag=after or name + "_codes", align_bytes=64)[:]
+            scales = sb.tile([P, width], U8, name=name + "_scales", align_bytes=64)
+            nc.vector.quantize_mx(out=codes.bitcast(FP8X4), scales=scales[:], in_=grouped)
+            return codes, scales
+
+        def interleave(name, raw, width, copy=nc.scalar.copy):
+            grouped = sb.tile([P, width * PACK], BF16, name=name + "_grouped", align_bytes=64)
+            copy(
+                out=grouped[:].rearrange("p (c i t) -> p c t i", i=4, t=PACK),
+                in_=raw[:].rearrange("p t (c i) -> p c t i", i=4),
+            )
+            return grouped
+
+        def turn(name, rows, after=None):
+            words = rows[:].bitcast(F32)
+            turned = ps2.tile([P, 2, P], F32, name=name + "_turned", tag="turned")
+            for u in range(2):
+                nc.tensor.transpose(turned[:, u, :], words[:, u : J // 2 : 2], ident[:])
+            grouped = sb.tile([P, P * PACK], BF16, name=name + "_grouped", tag=after or name + "_grouped", align_bytes=64)
+            nc.scalar.copy(
+                out=grouped[:].bitcast(F32).rearrange("p (x u) -> p x u", u=2),
+                in_=turned[:].rearrange("p u x -> p x u"),
+            )
+            return grouped
+
+        offsets = sb.tile([P, J // 16], U16, name="offsets")
+        nc.sync.dma_start(offsets[:], offs)
+        w1_raw = sb.tile([P, PACK, R], F32, name="w1_raw")
+        nc.sync.dma_start(w1_raw[:], w1.rearrange("(p t) r -> p t r", t=PACK))
+        scale_window = sb.tile([P, T], U8, name="scale_window", align_bytes=64)
+        nc.gpsimd.memset(scale_window[:].bitcast(I32), 0)
+        for q in range(4):
+            nc.sync.dma_start(scale_window[32 * q : 32 * q + 4, :].bitcast(I32), tab_scales[0, 4 * q : 4 * q + 4, :].bitcast(I32))
+        word_window = sb.tile([P, T], U16, name="word_window")
+        nc.sync.dma_start(word_window[:].bitcast(I32), tab_words[0].bitcast(I32))
+        wo_raw = sb.tile([P, PACK, R], F32, name="wo_raw")
+        nc.sync.dma_start(wo_raw[:], wo.rearrange("(p t) r -> p t r", t=PACK))
+        dy_raw = sb.tile([P, PACK, G], F32, name="dy_raw", align_bytes=64)
+        nc.sync.dma_start(dy_raw[:], dy.rearrange("(p t) g -> p t g", t=PACK))
+        x_planes = xrows.rearrange("(p c) t -> c p t", c=PACK)
+        x_windows = [sb.tile([P, T], F32, name="x_window%d" % c, align_bytes=64) for c in range(PACK)]
+        nc.sync.dma_start(x_windows[0][:], x_planes[0])
+        js_cols = sb.tile([P, PACK], F32, name="js_cols")
+        share_col = sb.tile([P, 1], F32, name="share_col")
+        with nc.allow_non_contiguous_dma(reason="one value of share to a partition"):
+            nc.sync.dma_start(js_cols[:], js.rearrange("o (p t) -> p (o t)", t=PACK))
+            nc.sync.dma_start(share_col[:], share)
+        for c in range(1, PACK):
+            nc.sync.dma_start(x_windows[c][:], x_planes[c])
+        old_sb = sb.tile([P, PACK, R], F32, name="old_sb")
+        nc.sync.dma_start(old_sb[:], old.rearrange("(p c) r -> p c r", c=PACK))
+
+        ident = sb.tile([P, P], F32, name="ident")
+        make_identity(nc, ident[:])
+
+        warm_in = sb.tile([P, 1], F32, name="warm_in")
+        warm_out = sb.tile([P, 1], F32, name="warm_out")
+        nc.vector.memset(warm_in[:], 1.0)
+        nc.scalar.activation(warm_out[:], warm_in[:], ACT.Abs_reciprocal_sqrt)
+
+        w1_codes, w1_scales = quantise("w1", interleave("w1", w1_raw, R, nc.vector.tensor_copy)[:], R)
+        a_half = []
+        for h in range(2):
+            tab_sc = sb.tile([P, HALF], U8, name="tab_sc%d" % h, tag="tab_sc", align_bytes=64)
+            nc.vector.tensor_copy(tab_sc[:], scale_window[:].indirect(offsets[:, h * 16 : (h + 1) * 16]))
+            tab_w = sb.tile([P, HALF], U16, name="tab_w%d" % h, align_bytes=64)
+            nc.vector.tensor_copy(tab_w[:], word_window[:].indirect(offsets[:, h * 16 : (h + 1) * 16]))
+            a = ps.tile([P, HALF], F32, name="a%d" % h)
+            nc.tensor.matmul_mx(
+                out=a[:], lhsT=w1_codes.bitcast(FP8X4), lhsT_scale=w1_scales[:],
+                rhs=tab_w[:].bitcast(FP4X4), rhs_scale=tab_sc[:], start=True, stop=True)
+            a_half.append(a)
+
+        wo_codes, wo_scales = quantise("wo", interleave("wo", wo_raw, R)[:], R)
+        dy_codes, dy_scales = quantise("dy", interleave("dy", dy_raw, G)[:], G)
+        c0 = ps.tile([P, G], F32, name="c0")
+        nc.tensor.matmul_mx(out=c0[:], lhsT=wo_codes.bitcast(FP8X4), lhsT_scale=wo_scales[:],
+                            rhs=dy_codes.bitcast(FP8X4), rhs_scale=dy_scales[:], start=True, stop=True)
+
+        js_rows = ps.tile([P, J], F32, name="js_rows")
+        for t in range(PACK):
+            nc.tensor.transpose(js_rows[:, t:J:PACK], js_cols[:, t : t + 1].to_broadcast([P, P]), ident[:])
+
+        squares = sb.tile([P, J], F32, name="squares")
+        sums = sb.tile([P, G], F32, name="sums")
+        GH = G // 2
+        square_sums = sb.tile([P, G], F32, name="square_sums")
+        for h in range(2):
+            nc.scalar.activation(squares[:, h * HALF : (h + 1) * HALF], a_half[h][:], ACT.Square)
+            nc.vector.tensor_reduce(sums[:, h * GH : (h + 1) * GH], a_half[h][:].rearrange("p (g i) -> p g i", i=GROUP), AX.X, ALU.add)
+            nc.vector.tensor_reduce(square_sums[:, h * GH : (h + 1) * GH], squares[:, h * HALF : (h + 1) * HALF].rearrange("p (g i) -> p g i", i=GROUP), AX.X, ALU.add)
+        mean_sq = sb.tile([P, G], F32, name="mean_sq")
+        nc.scalar.activation(mean_sq[:], sums[:], ACT.Square, scale=1.0 / GROUP)
+        mean = sb.tile([P, G], F32, name="mean")
+        nc.scalar.activation(mean[:], sums[:], ACT.Copy, scale=1.0 / GROUP)
+        var = sb.tile([P, G], F32, name="var")
+        nc.vector.scalar_tensor_tensor(var[:], square_sums[:], 1.0 / GROUP, mean_sq[:], ALU.mult, ALU.subtract)
+        inv_spread = sb.tile([P, G], F32, name="inv_spread", tag="dy_raw", align_bytes=64)
+        nc.scalar.activation(inv_spread[:], var[:], ACT.Abs_reciprocal_sqrt, bias=EPS)
+        x_listed = [sb.tile([P, J], BF16, name="x_listed0")]
+        nc.vector.tensor_copy(x_listed[0][:], x_windows[0][:].indirect(offsets[:]))
+        spread = sb.tile([P, G], F32, name="spread", tag="x_window0", align_bytes=64)
+        nc.vector.scalar_tensor_tensor(spread[:], var[:], EPS, inv_spread[:], ALU.add, ALU.mult)
+        z = sb.tile([P, G], F32, name="z", align_bytes=64)
+        nc.vector.scalar_tensor_tensor(z[:], mean[:], share_col[:, 0:1], spread[:], ALU.mult, ALU.add)
+        u = sb.tile([P, G], F32, name="u")
+        nc.scalar.activation(u[:], z[:], ACT.Tanh)
+        u_sq = sb.tile([P, G], F32, name="u_sq")
+        nc.scalar.activation(u_sq[:], u[:], ACT.Square)
+        shift = sb.tile([P, G], F32, name="shift")
+        nc.vector.scalar_tensor_tensor(shift[:], spread[:], share_col[:, 0:1], mean[:], ALU.mult, ALU.subtract)
+        shifted = sb.tile([P, J], F32, name="shifted")
+        for h in range(2):
+            nc.vector.tensor_tensor(
+                shifted[:, h * HALF : (h + 1) * HALF].rearrange("p (g i) -> p g i", i=GROUP),
+                a_half[h][:].rearrange("p (g i) -> p g i", i=GROUP),
+                shift[:, h * GH : (h + 1) * GH].unsqueeze(2).to_broadcast([P, GH, GROUP]), ALU.add)
+        scaled = sb.tile([P, J], F32, name="scaled", align_bytes=64)
+        nc.vector.tensor_tensor(scaled[:], js_rows[:], shifted[:], ALU.mult)
+
+        neg_gain = sb.tile([P, G], F32, name="neg_gain")
+        nc.vector.scalar_tensor_tensor(neg_gain[:], c0[:], -1.0 / GROUP, inv_spread[:], ALU.mult, ALU.mult)
+        gain = sb.tile([P, G], F32, name="gain")
+        nc.vector.scalar_tensor_tensor(gain[:], u_sq[:], 1.0, neg_gain[:], ALU.subtract, ALU.mult)
+        gs = sb.tile([P, J], BF16, name="gs")
+        nc.vector.tensor_tensor(
+            gs[:].rearrange("p (g i) -> p g i", i=GROUP),
+            scaled[:].rearrange("p (g i) -> p g i", i=GROUP),
+            gain[:].unsqueeze(2).to_broadcast([P, G, GROUP]), ALU.mult)
+        g_grouped = turn("g", gs)
+        x_grouped = [turn("x0", x_listed[0], after="z")]
+        x_listed.append(sb.tile([P, J], BF16, name="x_listed1", tag="scaled", align_bytes=64))
+        nc.vector.tensor_copy(x_listed[1][:], x_windows[1][:].indirect(offsets[:]))
+        pair_codes = sb.tile([P, 2 * P], U32, name="pair_codes", tag="x_window1", align_bytes=64)
+        x_q = [quantise("x0", x_grouped[0][:], P, codes=pair_codes[:, 0:P])]
+        g_codes, g_scales = quantise("g", g_grouped[:], R, codes=pair_codes[:, P : 2 * P])
+        for c in range(1, PACK):
+            x_grouped.append(turn("x%d" % c, x_listed[c]))
+            if c + 1 < PACK:
+                x_listed.append(sb.tile([P, J], BF16, name="x_listed%d" % (c + 1)))
+                nc.vector.tensor_copy(x_listed[c + 1][:], x_windows[c + 1][:].indirect(offsets[:]))
+            x_q.append(quantise("x%d" % c, x_grouped[c][:], P, after="x_window%d" % (c + 1) if c + 1 < PACK else None))
+
+        result = sb.tile([P, PACK, R], F32, name="result")
+        out_rows = out.rearrange("(p c) r -> p c r", c=PACK)
+        for name, c0_, c1_ in (("gw_first", 0, PACK - 1), ("gw_last", PACK - 1, PACK)):
+            gw = ps.tile([P, c1_ - c0_, R], F32, name=name)
+            for c in range(c0_, c1_):
+                nc.tensor.matmul_mx(out=gw[:, c - c0_, :], lhsT=x_q[c][0].bitcast(FP8X4), lhsT_scale=x_q[c][1][:],
+                                    rhs=g_codes.bitcast(FP8X4), rhs_scale=g_scales[:], start=True, stop=True)
+            nc.vector.tensor_tensor(result[:, c0_:c1_, :], gw[:], old_sb[:, c0_:c1_, :], ALU.add)
+            nc.sync.dma_start(out_rows[:, c0_:c1_, :], result[:, c0_:c1_, :])

@@ -28,6 +28,7 @@ def tile_attend_cspreadpool_w_kernel(tc, tab_words, tab_scales, w1, share, wo, d
     nc = tc.nc
     with ExitStack() as ctx:
         sb = ctx.enter_context(tc.tile_pool(name="sb", bufs=1))
+        last = ctx.enter_context(tc.tile_pool(name="last", bufs=1))
         ps = ctx.enter_context(tc.psum_pool(name="ps", bufs=1))
         ps2 = ctx.enter_context(tc.psum_pool(name="ps2", bufs=2))
 
@@ -46,142 +47,150 @@ def tile_attend_cspreadpool_w_kernel(tc, tab_words, tab_scales, w1, share, wo, d
             )
             return grouped
 
-        def turn(name, rows, after=None):
+        def turn(name, rows, grouped):
             words = rows[:].bitcast(F32)
             turned = ps2.tile([P, 2, P], F32, name=name + "_turned", tag="turned")
             for u in range(2):
                 nc.tensor.transpose(turned[:, u, :], words[:, u : J // 2 : 2], ident[:])
-            grouped = sb.tile([P, P * PACK], BF16, name=name + "_grouped", tag=after or name + "_grouped", align_bytes=64)
             nc.scalar.copy(
-                out=grouped[:].bitcast(F32).rearrange("p (x u) -> p x u", u=2),
+                out=grouped.bitcast(F32).rearrange("p (x u) -> p x u", u=2),
                 in_=turned[:].rearrange("p u x -> p x u"),
             )
-            return grouped
 
         offsets = sb.tile([P, J // 16], U16, name="offsets")
         nc.sync.dma_start(offsets[:], offs)
         w1_raw = sb.tile([P, PACK, R], F32, name="w1_raw")
         nc.sync.dma_start(w1_raw[:], w1.rearrange("(p t) r -> p t r", t=PACK))
-        scale_window = sb.tile([P, T], U8, name="scale_window", align_bytes=64)
+        scale_window = sb.tile([P, T], U8, name="scale_window")
         nc.gpsimd.memset(scale_window[:].bitcast(I32), 0)
         for q in range(4):
             nc.sync.dma_start(scale_window[32 * q : 32 * q + 4, :].bitcast(I32), tab_scales[0, 4 * q : 4 * q + 4, :].bitcast(I32))
         word_window = sb.tile([P, T], U16, name="word_window")
         nc.sync.dma_start(word_window[:].bitcast(I32), tab_words[0].bitcast(I32))
+        x_planes = xrows.rearrange("(p c) t -> c p t", c=PACK)
+        x_windows = [sb.tile([P, T], F32, name="x_window%d" % c, align_bytes=64) for c in range(PACK - 1)]
+        x_windows.append(last.tile([P, T], F32, name="x_window3", align_bytes=64, offset=0))
+        js_cols = sb.tile([P, PACK], F32, name="js_cols")
+        share_col = sb.tile([P, 1], F32, name="share_col")
+        nc.sync.dma_start(x_windows[0][:], x_planes[0])
         wo_raw = sb.tile([P, PACK, R], F32, name="wo_raw")
         nc.sync.dma_start(wo_raw[:], wo.rearrange("(p t) r -> p t r", t=PACK))
         dy_raw = sb.tile([P, PACK, G], F32, name="dy_raw", align_bytes=64)
         nc.sync.dma_start(dy_raw[:], dy.rearrange("(p t) g -> p t g", t=PACK))
-        x_planes = xrows.rearrange("(p c) t -> c p t", c=PACK)
-        x_windows = [sb.tile([P, T], F32, name="x_window%d" % c, align_bytes=64) for c in range(PACK)]
-        nc.sync.dma_start(x_windows[0][:], x_planes[0])
-        js_cols = sb.tile([P, PACK], F32, name="js_cols")
-        share_col = sb.tile([P, 1], F32, name="share_col")
         with nc.allow_non_contiguous_dma(reason="one value of share to a partition"):
-            nc.sync.dma_start(js_cols[:], js.rearrange("o (p t) -> p (o t)", t=PACK))
             nc.sync.dma_start(share_col[:], share)
-        for c in range(1, PACK):
+        nc.sync.dma_start(x_windows[1][:], x_planes[1])
+        nc.sync.dma_start(js_cols[:], js.rearrange("o (p t) -> p (o t)", t=PACK))
+        for c in range(2, PACK):
             nc.sync.dma_start(x_windows[c][:], x_planes[c])
         old_sb = sb.tile([P, PACK, R], F32, name="old_sb")
         nc.sync.dma_start(old_sb[:], old.rearrange("(p c) r -> p c r", c=PACK))
-
-        ident = sb.tile([P, P], F32, name="ident")
-        make_identity(nc, ident[:])
 
         warm_in = sb.tile([P, 1], F32, name="warm_in")
         warm_out = sb.tile([P, 1], F32, name="warm_out")
         nc.vector.memset(warm_in[:], 1.0)
         nc.scalar.activation(warm_out[:], warm_in[:], ACT.Abs_reciprocal_sqrt)
 
+        ident = sb.tile([P, P], F32, name="ident")
+        make_identity(nc, ident[:])
+
         w1_codes, w1_scales = quantise("w1", interleave("w1", w1_raw, R, nc.vector.tensor_copy)[:], R)
+        tab_sc = sb.tile([P, J], U8, name="tab_sc", align_bytes=64)
+        nc.vector.tensor_copy(tab_sc[:], scale_window[:].indirect(offsets[:]))
         a_half = []
         for h in range(2):
-            tab_sc = sb.tile([P, HALF], U8, name="tab_sc%d" % h, tag="tab_sc", align_bytes=64)
-            nc.vector.tensor_copy(tab_sc[:], scale_window[:].indirect(offsets[:, h * 16 : (h + 1) * 16]))
             tab_w = sb.tile([P, HALF], U16, name="tab_w%d" % h, align_bytes=64)
             nc.vector.tensor_copy(tab_w[:], word_window[:].indirect(offsets[:, h * 16 : (h + 1) * 16]))
             a = ps.tile([P, HALF], F32, name="a%d" % h)
             nc.tensor.matmul_mx(
                 out=a[:], lhsT=w1_codes.bitcast(FP8X4), lhsT_scale=w1_scales[:],
-                rhs=tab_w[:].bitcast(FP4X4), rhs_scale=tab_sc[:], start=True, stop=True)
+                rhs=tab_w[:].bitcast(FP4X4), rhs_scale=tab_sc[:, h * HALF : (h + 1) * HALF], start=True, stop=True)
             a_half.append(a)
 
+        def gather_x(c):
+            listed = sb.tile([P, J], BF16, name="x_listed%d" % c)
+            nc.vector.tensor_copy(listed[:], x_windows[c][:].indirect(offsets[:]))
+            return listed
+
+        x_listed = [gather_x(0)]
+
+        GH = G // 2
+        powers = sb.tile([P, 2, J], F32, name="powers")
+        a_sb = powers[:, 0, :]
+        power_sums = sb.tile([P, 2, G], F32, name="power_sums", tag="x_window0", align_bytes=64)
+        sums = power_sums[:, 0, :]
+        for h in range(2):
+            slots = slice(h * HALF, (h + 1) * HALF)
+            nc.scalar.copy(powers[:, 0, slots], a_half[h][:])
+            nc.scalar.activation(powers[:, 1, slots], a_half[h][:], ACT.Square)
+        nc.vector.tensor_reduce(power_sums[:, :, 0:GH], powers[:, :, 0:HALF].rearrange("p e (g i) -> p e g i", i=GROUP), AX.X, ALU.add)
+        for e in range(2):
+            nc.vector.tensor_reduce(power_sums[:, e, GH:G], powers[:, e, HALF:J].rearrange("p (g i) -> p g i", i=GROUP), AX.X, ALU.add)
+        mean_sq = sb.tile([P, G], F32, name="mean_sq")
+        nc.vector.scalar_tensor_tensor(mean_sq[:], sums, 1.0 / GROUP**2, sums, ALU.mult, ALU.mult)
+        mean = sb.tile([P, G], F32, name="mean")
+        nc.vector.tensor_scalar(mean[:], sums, 1.0 / GROUP, None, ALU.mult)
+        var = sb.tile([P, G], F32, name="var")
+        nc.vector.scalar_tensor_tensor(var[:], power_sums[:, 1, :], 1.0 / GROUP, mean_sq[:], ALU.mult, ALU.subtract)
         wo_codes, wo_scales = quantise("wo", interleave("wo", wo_raw, R)[:], R)
         dy_codes, dy_scales = quantise("dy", interleave("dy", dy_raw, G)[:], G)
         c0 = ps.tile([P, G], F32, name="c0")
         nc.tensor.matmul_mx(out=c0[:], lhsT=wo_codes.bitcast(FP8X4), lhsT_scale=wo_scales[:],
                             rhs=dy_codes.bitcast(FP8X4), rhs_scale=dy_scales[:], start=True, stop=True)
 
-        js_rows = ps.tile([P, J], F32, name="js_rows")
-        for t in range(PACK):
-            nc.tensor.transpose(js_rows[:, t:J:PACK], js_cols[:, t : t + 1].to_broadcast([P, P]), ident[:])
-
-        squares = sb.tile([P, J], F32, name="squares")
-        sums = sb.tile([P, G], F32, name="sums")
-        GH = G // 2
-        square_sums = sb.tile([P, G], F32, name="square_sums")
-        for h in range(2):
-            nc.scalar.activation(squares[:, h * HALF : (h + 1) * HALF], a_half[h][:], ACT.Square)
-            nc.vector.tensor_reduce(sums[:, h * GH : (h + 1) * GH], a_half[h][:].rearrange("p (g i) -> p g i", i=GROUP), AX.X, ALU.add)
-            nc.vector.tensor_reduce(square_sums[:, h * GH : (h + 1) * GH], squares[:, h * HALF : (h + 1) * HALF].rearrange("p (g i) -> p g i", i=GROUP), AX.X, ALU.add)
-        mean_sq = sb.tile([P, G], F32, name="mean_sq")
-        nc.scalar.activation(mean_sq[:], sums[:], ACT.Square, scale=1.0 / GROUP)
-        mean = sb.tile([P, G], F32, name="mean")
-        nc.scalar.activation(mean[:], sums[:], ACT.Copy, scale=1.0 / GROUP)
-        var = sb.tile([P, G], F32, name="var")
-        nc.vector.scalar_tensor_tensor(var[:], square_sums[:], 1.0 / GROUP, mean_sq[:], ALU.mult, ALU.subtract)
         inv_spread = sb.tile([P, G], F32, name="inv_spread", tag="dy_raw", align_bytes=64)
         nc.scalar.activation(inv_spread[:], var[:], ACT.Abs_reciprocal_sqrt, bias=EPS)
-        x_listed = [sb.tile([P, J], BF16, name="x_listed0")]
-        nc.vector.tensor_copy(x_listed[0][:], x_windows[0][:].indirect(offsets[:]))
-        spread = sb.tile([P, G], F32, name="spread", tag="x_window0", align_bytes=64)
+        shifted = ps.tile([P, PACK, R], F32, name="shifted")
+        for t in range(PACK):
+            nc.tensor.matmul(shifted[:, t, :], a_sb[:, t:J:PACK], ident[:], start=(t == 0), stop=False, is_transpose=True)
+
+        def twice(tile):
+            return tile[:].unsqueeze(2).to_broadcast([P, G, 2])
+
+        spread = sb.tile([P, G], F32, name="spread")
         nc.vector.scalar_tensor_tensor(spread[:], var[:], EPS, inv_spread[:], ALU.add, ALU.mult)
+        neg_gain = sb.tile([P, G], F32, name="neg_gain")
+        nc.vector.scalar_tensor_tensor(neg_gain[:], c0[:], -1.0 / GROUP, inv_spread[:], ALU.mult, ALU.mult)
         z = sb.tile([P, G], F32, name="z", align_bytes=64)
         nc.vector.scalar_tensor_tensor(z[:], mean[:], share_col[:, 0:1], spread[:], ALU.mult, ALU.add)
         u = sb.tile([P, G], F32, name="u")
         nc.scalar.activation(u[:], z[:], ACT.Tanh)
         u_sq = sb.tile([P, G], F32, name="u_sq")
         nc.scalar.activation(u_sq[:], u[:], ACT.Square)
-        shift = sb.tile([P, G], F32, name="shift")
-        nc.vector.scalar_tensor_tensor(shift[:], spread[:], share_col[:, 0:1], mean[:], ALU.mult, ALU.subtract)
-        shifted = sb.tile([P, J], F32, name="shifted")
-        for h in range(2):
-            nc.vector.tensor_tensor(
-                shifted[:, h * HALF : (h + 1) * HALF].rearrange("p (g i) -> p g i", i=GROUP),
-                a_half[h][:].rearrange("p (g i) -> p g i", i=GROUP),
-                shift[:, h * GH : (h + 1) * GH].unsqueeze(2).to_broadcast([P, GH, GROUP]), ALU.add)
-        scaled = sb.tile([P, J], F32, name="scaled", align_bytes=64)
-        nc.vector.tensor_tensor(scaled[:], js_rows[:], shifted[:], ALU.mult)
-
-        neg_gain = sb.tile([P, G], F32, name="neg_gain")
-        nc.vector.scalar_tensor_tensor(neg_gain[:], c0[:], -1.0 / GROUP, inv_spread[:], ALU.mult, ALU.mult)
-        gain = sb.tile([P, G], F32, name="gain")
-        nc.vector.scalar_tensor_tensor(gain[:], u_sq[:], 1.0, neg_gain[:], ALU.subtract, ALU.mult)
-        gs = sb.tile([P, J], BF16, name="gs")
+        shift = sb.tile([P, G, 2], F32, name="shift")
+        nc.vector.scalar_tensor_tensor(shift[:], twice(spread), share_col[:, 0:1], twice(mean), ALU.mult, ALU.subtract)
+        for t in range(PACK):
+            nc.tensor.matmul(shifted[:, t, :], shift[:].rearrange("p g e -> p (g e)"), ident[:], start=False, stop=(t == PACK - 1), is_transpose=True)
+        scaled = sb.tile([P, PACK, R], F32, name="scaled")
+        for t in range(PACK):
+            nc.scalar.activation(scaled[:, t, :], shifted[:, t, :], ACT.Copy, scale=js_cols[:, t : t + 1])
+        x_listed.append(gather_x(1))
+        x_listed.append(gather_x(2))
+        gain = sb.tile([P, G, 2], F32, name="gain", tag="x_window2", align_bytes=64)
+        nc.vector.scalar_tensor_tensor(gain[:], twice(u_sq), 1.0, twice(neg_gain), ALU.subtract, ALU.mult)
+        gain_turned = ps.tile([P, R], F32, name="gain_turned", tag="c0")
+        nc.tensor.transpose(gain_turned[:], gain[:].rearrange("p g e -> p (g e)"), ident[:])
+        x_listed.append(gather_x(3))
+        g_grouped = last.tile([P, J], BF16, name="g_grouped", align_bytes=64, offset=0)[:]
+        x01_codes = last.tile([P, 2 * P], U32, name="x01_codes", align_bytes=64, offset=2 * J)
         nc.vector.tensor_tensor(
-            gs[:].rearrange("p (g i) -> p g i", i=GROUP),
-            scaled[:].rearrange("p (g i) -> p g i", i=GROUP),
-            gain[:].unsqueeze(2).to_broadcast([P, G, GROUP]), ALU.mult)
-        g_grouped = turn("g", gs)
-        x_grouped = [turn("x0", x_listed[0], after="z")]
-        x_listed.append(sb.tile([P, J], BF16, name="x_listed1", tag="scaled", align_bytes=64))
-        nc.vector.tensor_copy(x_listed[1][:], x_windows[1][:].indirect(offsets[:]))
-        pair_codes = sb.tile([P, 2 * P], U32, name="pair_codes", tag="x_window1", align_bytes=64)
-        x_q = [quantise("x0", x_grouped[0][:], P, codes=pair_codes[:, 0:P])]
-        g_codes, g_scales = quantise("g", g_grouped[:], R, codes=pair_codes[:, P : 2 * P])
-        for c in range(1, PACK):
-            x_grouped.append(turn("x%d" % c, x_listed[c]))
-            if c + 1 < PACK:
-                x_listed.append(sb.tile([P, J], BF16, name="x_listed%d" % (c + 1)))
-                nc.vector.tensor_copy(x_listed[c + 1][:], x_windows[c + 1][:].indirect(offsets[:]))
-            x_q.append(quantise("x%d" % c, x_grouped[c][:], P, after="x_window%d" % (c + 1) if c + 1 < PACK else None))
+            g_grouped.rearrange("p (r t) -> p r t", t=PACK),
+            gain_turned[:].unsqueeze(2).to_broadcast([P, R, PACK]), scaled[:].rearrange("p t r -> p r t"), ALU.mult)
+        x_grouped = [sb.tile([P, 2 * J], BF16, name="x_grouped%d" % pair, align_bytes=64) for pair in range(2)]
+        for c in range(PACK):
+            turn("x%d" % c, x_listed[c], x_grouped[c // 2][:, (c % 2) * J : (c % 2 + 1) * J])
+        x_q = [quantise("x01", x_grouped[0][:], 2 * P, codes=x01_codes[:])]
+        g_codes, g_scales = quantise("g", g_grouped, R)
+        x_q.append(quantise("x23", x_grouped[1][:], 2 * P))
 
         result = sb.tile([P, PACK, R], F32, name="result")
         out_rows = out.rearrange("(p c) r -> p c r", c=PACK)
-        for name, c0_, c1_ in (("gw_first", 0, PACK - 1), ("gw_last", PACK - 1, PACK)):
-            gw = ps.tile([P, c1_ - c0_, R], F32, name=name)
-            for c in range(c0_, c1_):
-                nc.tensor.matmul_mx(out=gw[:, c - c0_, :], lhsT=x_q[c][0].bitcast(FP8X4), lhsT_scale=x_q[c][1][:],
+        for pair in range(2):
+            planes = slice(2 * pair, 2 * pair + 2)
+            gw = ps.tile([P, 2, R], F32, name="gw%d" % pair)
+            x_codes, x_scales = x_q[pair]
+            for e in range(2):
+                nc.tensor.matmul_mx(out=gw[:, e, :], lhsT=x_codes[:, e * P : (e + 1) * P].bitcast(FP8X4), lhsT_scale=x_scales[:, e * P : (e + 1) * P],
                                     rhs=g_codes.bitcast(FP8X4), rhs_scale=g_scales[:], start=True, stop=True)
-            nc.vector.tensor_tensor(result[:, c0_:c1_, :], gw[:], old_sb[:, c0_:c1_, :], ALU.add)
-            nc.sync.dma_start(out_rows[:, c0_:c1_, :], result[:, c0_:c1_, :])
+            nc.vector.tensor_tensor(result[:, planes, :], gw[:], old_sb[:, planes, :], ALU.add)
+            nc.sync.dma_start(out_rows[:, planes, :], result[:, planes, :])

@@ -63,8 +63,8 @@ def tile_attend_cspreadpool_w_kernel(tc, tab_words, tab_scales, w1, share, wo, d
         nc.sync.dma_start(w1_raw[:], w1.rearrange("(p t) r -> p t r", t=PACK))
         scale_window = sb.tile([P, T], U8, name="scale_window")
         nc.gpsimd.memset(scale_window[:].bitcast(I32), 0)
-        for q in range(4):
-            nc.sync.dma_start(scale_window[32 * q : 32 * q + 4, :].bitcast(I32), tab_scales[0, 4 * q : 4 * q + 4, :].bitcast(I32))
+        for f in range(4):
+            nc.sync.dma_start(scale_window[f:P:32, :].bitcast(I32), tab_scales[0, f:16:4, :].bitcast(I32))
         word_window = sb.tile([P, T], U16, name="word_window")
         nc.sync.dma_start(word_window[:].bitcast(I32), tab_words[0].bitcast(I32))
         x_planes = xrows.rearrange("(p c) t -> c p t", c=PACK)
@@ -174,8 +174,9 @@ def tile_attend_cspreadpool_w_kernel(tc, tab_words, tab_scales, w1, share, wo, d
         g_grouped = last.tile([P, J], BF16, name="g_grouped", align_bytes=64, offset=0)[:]
         x01_codes = last.tile([P, 2 * P], U32, name="x01_codes", align_bytes=64, offset=2 * J)
         nc.vector.tensor_tensor(
-            g_grouped.rearrange("p (r t) -> p r t", t=PACK),
-            gain_turned[:].unsqueeze(2).to_broadcast([P, R, PACK]), scaled[:].rearrange("p t r -> p r t"), ALU.mult)
+            g_grouped.rearrange("p (c i t) -> p c t i", i=4, t=PACK),
+            gain_turned[:].rearrange("p (c i) -> p c i", i=4).unsqueeze(2).to_broadcast([P, R // 4, PACK, 4]),
+            scaled[:].rearrange("p t (c i) -> p c t i", i=4), ALU.mult)
         x_grouped = [sb.tile([P, 2 * J], BF16, name="x_grouped%d" % pair, align_bytes=64) for pair in range(2)]
         for c in range(PACK):
             turn("x%d" % c, x_listed[c], x_grouped[c // 2][:, (c % 2) * J : (c % 2 + 1) * J])

@@ -77,10 +77,7 @@ def tile_attend_cspreadpool_w_kernel(tc, tab_words, tab_scales, w1, share, wo, d
         nc.sync.dma_start(wo_raw[:], wo.rearrange("(p t) r -> p t r", t=PACK))
         dy_raw = sb.tile([P, PACK, G], F32, name="dy_raw", align_bytes=64)
         nc.sync.dma_start(dy_raw[:], dy.rearrange("(p t) g -> p t g", t=PACK))
-        with nc.allow_non_contiguous_dma(reason="one value of share to a partition"):
-            nc.sync.dma_start(share_col[:], share)
         nc.sync.dma_start(x_windows[1][:], x_planes[1])
-        nc.sync.dma_start(js_cols[:], js.rearrange("o (p t) -> p (o t)", t=PACK))
         for c in range(2, PACK):
             nc.sync.dma_start(x_windows[c][:], x_planes[c])
         old_sb = sb.tile([P, PACK, R], F32, name="old_sb")
@@ -93,6 +90,9 @@ def tile_attend_cspreadpool_w_kernel(tc, tab_words, tab_scales, w1, share, wo, d
 
         ident = sb.tile([P, P], F32, name="ident")
         make_identity(nc, ident[:])
+        with nc.allow_non_contiguous_dma(reason="one value of share to a partition"):
+            nc.gpsimd.dma_start(share_col[:], share)
+        nc.gpsimd.dma_start(js_cols[:], js.rearrange("o (p t) -> p (o t)", t=PACK))
 
         w1_codes, w1_scales = quantise("w1", interleave("w1", w1_raw, R, nc.vector.tensor_copy)[:], R)
         tab_sc = sb.tile([P, J], U8, name="tab_sc", align_bytes=64)

from contextlib import ExitStack

import concourse.mybir as mybir
from concourse.masks import make_identity

K, R, F, T, J, G = 512, 128, 512, 2048, 512, 64
GROUP = J // G
EPS = 0.05
P = 128
PACK = 4
HALF = J // 2
FLOPS = 2 * K * R * J + 2 * F * R * G + 2 * J * K * R

F32 = mybir.dt.float32
BF16 = mybir.dt.bfloat16
I32 = mybir.dt.int32
U32 = mybir.dt.uint32
U16 = mybir.dt.uint16
U8 = mybir.dt.uint8
FP8X4 = mybir.dt.float8_e4m3fn_x4
FP4X4 = mybir.dt.float4_e2m1fn_x4
ALU = mybir.AluOpType
ACT = mybir.ActivationFunctionType
AX = mybir.AxisListType


def tile_attend_cspreadpool_w_kernel(tc, tab_words, tab_scales, w1, share, wo, dy, js, xrows, old, offs, out):
    nc = tc.nc
    with ExitStack() as ctx:
        sb = ctx.enter_context(tc.tile_pool(name="sb", bufs=1))
        last = ctx.enter_context(tc.tile_pool(name="last", bufs=1))
        ps = ctx.enter_context(tc.psum_pool(name="ps", bufs=1))
        ps2 = ctx.enter_context(tc.psum_pool(name="ps2", bufs=2))

        def quantise(name, grouped, width, after=None, codes=None):
            if codes is None:
                codes = sb.tile([P, width], U32, name=name + "_codes", tag=after or name + "_codes", align_bytes=64)[:]
            scales = sb.tile([P, width], U8, name=name + "_scales", align_bytes=64)
            nc.vector.quantize_mx(out=codes.bitcast(FP8X4), scales=scales[:], in_=grouped)
            return codes, scales

        def interleave(name, raw, width, copy=nc.scalar.copy):
            grouped = sb.tile([P, width * PACK], BF16, name=name + "_grouped", align_bytes=64)
            copy(
                out=grouped[:].rearrange("p (c i t) -> p c t i", i=4, t=PACK),
                in_=raw[:].rearrange("p t (c i) -> p c t i", i=4),
            )
            return grouped

        def turn(name, rows, grouped):
            words = rows[:].bitcast(F32)
            turned = ps2.tile([P, 2, P], F32, name=name + "_turned", tag="turned")
            for u in range(2):
                nc.tensor.transpose(turned[:, u, :], words[:, u : J // 2 : 2], ident[:])
            nc.scalar.copy(
                out=grouped.bitcast(F32).rearrange("p (x u) -> p x u", u=2),
                in_=turned[:].rearrange("p u x -> p x u"),
            )

        offsets = sb.tile([P, J // 16], U16, name="offsets")
        nc.sync.dma_start(offsets[:], offs)
        w1_raw = sb.tile([P, PACK, R], F32, name="w1_raw")
        nc.sync.dma_start(w1_raw[:], w1.rearrange("(p t) r -> p t r", t=PACK))
        scale_window = sb.tile([P, T], U8, name="scale_window")
        nc.gpsimd.memset(scale_window[:].bitcast(I32), 0)
        for f in range(4):
            nc.sync.dma_start(scale_window[f:P:32, :].bitcast(I32), tab_scales[0, f:16:4, :].bitcast(I32))
        word_window = sb.tile([P, T], U16, name="word_window")
        nc.sync.dma_start(word_window[:].bitcast(I32), tab_words[0].bitcast(I32))
        x_planes = xrows.rearrange("(p c) t -> c p t", c=PACK)
        x_windows = [sb.tile([P, T], F32, name="x_window%d" % c, align_bytes=64) for c in range(PACK - 1)]
        x_windows.append(last.tile([P, T], F32, name="x_window3", align_bytes=64, offset=0))
        js_cols = sb.tile([P, PACK], F32, name="js_cols")
        share_col = sb.tile([P, 1], F32, name="share_col")
        nc.sync.dma_start(x_windows[0][:], x_planes[0])
        wo_raw = sb.tile([P, PACK, R], F32, name="wo_raw")
        nc.sync.dma_start(wo_raw[:], wo.rearrange("(p t) r -> p t r", t=PACK))
        dy_raw = sb.tile([P, PACK, G], F32, name="dy_raw", align_bytes=64)
        nc.sync.dma_start(dy_raw[:], dy.rearrange("(p t) g -> p t g", t=PACK))
        nc.sync.dma_start(x_windows[1][:], x_planes[1])
        for c in range(2, PACK):
            nc.sync.dma_start(x_windows[c][:], x_planes[c])
        old_sb = sb.tile([P, PACK, R], F32, name="old_sb")
        nc.sync.dma_start(old_sb[:], old.rearrange("(p c) r -> p c r", c=PACK))

        warm_in = sb.tile([P, 1], F32, name="warm_in")
        warm_out = sb.tile([P, 1], F32, name="warm_out")
        nc.vector.memset(warm_in[:], 1.0)
        nc.scalar.activation(warm_out[:], warm_in[:], ACT.Abs_reciprocal_sqrt)

        ident = sb.tile([P, P], F32, name="ident")
        make_identity(nc, ident[:])
        with nc.allow_non_contiguous_dma(reason="one value of share to a partition"):
            nc.gpsimd.dma_start(share_col[:], share)
        nc.gpsimd.dma_start(js_cols[:], js.rearrange("o (p t) -> p (o t)", t=PACK))

        w1_codes, w1_scales = quantise("w1", interleave("w1", w1_raw, R, nc.vector.tensor_copy)[:], R)
        tab_sc = sb.tile([P, J], U8, name="tab_sc", align_bytes=64)
        nc.vector.tensor_copy(tab_sc[:], scale_window[:].indirect(offsets[:]))
        a_half = []
        for h in range(2):
            tab_w = sb.tile([P, HALF], U16, name="tab_w%d" % h, align_bytes=64)
            nc.vector.tensor_copy(tab_w[:], word_window[:].indirect(offsets[:, h * 16 : (h + 1) * 16]))
            a = ps.tile([P, HALF], F32, name="a%d" % h)
            nc.tensor.matmul_mx(
                out=a[:], lhsT=w1_codes.bitcast(FP8X4), lhsT_scale=w1_scales[:],
                rhs=tab_w[:].bitcast(FP4X4), rhs_scale=tab_sc[:, h * HALF : (h + 1) * HALF], start=True, stop=True)
            a_half.append(a)

        def gather_x(c):
            listed = sb.tile([P, J], BF16, name="x_listed%d" % c)
            nc.vector.tensor_copy(listed[:], x_windows[c][:].indirect(offsets[:]))
            return listed

        x_listed = [gather_x(0)]

        GH = G // 2
        powers = sb.tile([P, 2, J], F32, name="powers")
        a_sb = powers[:, 0, :]
        power_sums = sb.tile([P, 2, G], F32, name="power_sums", tag="x_window0", align_bytes=64)
        sums = power_sums[:, 0, :]
        for h in range(2):
            slots = slice(h * HALF, (h + 1) * HALF)
            nc.scalar.copy(powers[:, 0, slots], a_half[h][:])
            nc.scalar.activation(powers[:, 1, slots], a_half[h][:], ACT.Square)
        nc.vector.tensor_reduce(power_sums[:, :, 0:GH], powers[:, :, 0:HALF].rearrange("p e (g i) -> p e g i", i=GROUP), AX.X, ALU.add)
        for e in range(2):
            nc.vector.tensor_reduce(power_sums[:, e, GH:G], powers[:, e, HALF:J].rearrange("p (g i) -> p g i", i=GROUP), AX.X, ALU.add)
        mean_sq = sb.tile([P, G], F32, name="mean_sq")
        nc.vector.scalar_tensor_tensor(mean_sq[:], sums, 1.0 / GROUP**2, sums, ALU.mult, ALU.mult)
        mean = sb.tile([P, G], F32, name="mean")
        nc.vector.tensor_scalar(mean[:], sums, 1.0 / GROUP, None, ALU.mult)
        var = sb.tile([P, G], F32, name="var")
        nc.vector.scalar_tensor_tensor(var[:], power_sums[:, 1, :], 1.0 / GROUP, mean_sq[:], ALU.mult, ALU.subtract)
        wo_codes, wo_scales = quantise("wo", interleave("wo", wo_raw, R)[:], R)
        dy_codes, dy_scales = quantise("dy", interleave("dy", dy_raw, G)[:], G)
        c0 = ps.tile([P, G], F32, name="c0")
        nc.tensor.matmul_mx(out=c0[:], lhsT=wo_codes.bitcast(FP8X4), lhsT_scale=wo_scales[:],
                            rhs=dy_codes.bitcast(FP8X4), rhs_scale=dy_scales[:], start=True, stop=True)

        inv_spread = sb.tile([P, G], F32, name="inv_spread", tag="dy_raw", align_bytes=64)
        nc.scalar.activation(inv_spread[:], var[:], ACT.Abs_reciprocal_sqrt, bias=EPS)
        shifted = ps.tile([P, PACK, R], F32, name="shifted")
        for t in range(PACK):
            nc.tensor.matmul(shifted[:, t, :], a_sb[:, t:J:PACK], ident[:], start=(t == 0), stop=False, is_transpose=True)

        def twice(tile):
            return tile[:].unsqueeze(2).to_broadcast([P, G, 2])

        spread = sb.tile([P, G], F32, name="spread")
        nc.vector.scalar_tensor_tensor(spread[:], var[:], EPS, inv_spread[:], ALU.add, ALU.mult)
        neg_gain = sb.tile([P, G], F32, name="neg_gain")
        nc.vector.scalar_tensor_tensor(neg_gain[:], c0[:], -1.0 / GROUP, inv_spread[:], ALU.mult, ALU.mult)
        z = sb.tile([P, G], F32, name="z", align_bytes=64)
        nc.vector.scalar_tensor_tensor(z[:], mean[:], share_col[:, 0:1], spread[:], ALU.mult, ALU.add)
        u = sb.tile([P, G], F32, name="u")
        nc.scalar.activation(u[:], z[:], ACT.Tanh)
        u_sq = sb.tile([P, G], F32, name="u_sq")
        nc.scalar.activation(u_sq[:], u[:], ACT.Square)
        shift = sb.tile([P, G, 2], F32, name="shift")
        nc.vector.scalar_tensor_tensor(shift[:], twice(spread), share_col[:, 0:1], twice(mean), ALU.mult, ALU.subtract)
        for t in range(PACK):
            nc.tensor.matmul(shifted[:, t, :], shift[:].rearrange("p g e -> p (g e)"), ident[:], start=False, stop=(t == PACK - 1), is_transpose=True)
        scaled = sb.tile([P, PACK, R], F32, name="scaled")
        for t in range(PACK):
            nc.scalar.activation(scaled[:, t, :], shifted[:, t, :], ACT.Copy, scale=js_cols[:, t : t + 1])
        x_listed.append(gather_x(1))
        x_listed.append(gather_x(2))
        gain = sb.tile([P, G, 2], F32, name="gain", tag="x_window2", align_bytes=64)
        nc.vector.scalar_tensor_tensor(gain[:], twice(u_sq), 1.0, twice(neg_gain), ALU.subtract, ALU.mult)
        gain_turned = ps.tile([P, R], F32, name="gain_turned", tag="c0")
        nc.tensor.transpose(gain_turned[:], gain[:].rearrange("p g e -> p (g e)"), ident[:])
        x_listed.append(gather_x(3))
        g_grouped = last.tile([P, J], BF16, name="g_grouped", align_bytes=64, offset=0)[:]
        x01_codes = last.tile([P, 2 * P], U32, name="x01_codes", align_bytes=64, offset=2 * J)
        nc.vector.tensor_tensor(
            g_grouped.rearrange("p (c i t) -> p c t i", i=4, t=PACK),
            gain_turned[:].rearrange("p (c i) -> p c i", i=4).unsqueeze(2).to_broadcast([P, R // 4, PACK, 4]),
            scaled[:].rearrange("p t (c i) -> p c t i", i=4), ALU.mult)
        x_grouped = [sb.tile([P, 2 * J], BF16, name="x_grouped%d" % pair, align_bytes=64) for pair in range(2)]
        for c in range(PACK):
            turn("x%d" % c, x_listed[c], x_grouped[c // 2][:, (c % 2) * J : (c % 2 + 1) * J])
        x_q = [quantise("x01", x_grouped[0][:], 2 * P, codes=x01_codes[:])]
        g_codes, g_scales = quantise("g", g_grouped, R)
        x_q.append(quantise("x23", x_grouped[1][:], 2 * P))

        result = sb.tile([P, PACK, R], F32, name="result")
        out_rows = out.rearrange("(p c) r -> p c r", c=PACK)
        for pair in range(2):
            planes = slice(2 * pair, 2 * pair + 2)
            gw = ps.tile([P, 2, R], F32, name="gw%d" % pair)
            x_codes, x_scales = x_q[pair]
            for e in range(2):
                nc.tensor.matmul_mx(out=gw[:, e, :], lhsT=x_codes[:, e * P : (e + 1) * P].bitcast(FP8X4), lhsT_scale=x_scales[:, e * P : (e + 1) * P],
                                    rhs=g_codes.bitcast(FP8X4), rhs_scale=g_scales[:], start=True, stop=True)
            nc.vector.tensor_tensor(result[:, planes, :], gw[:], old_sb[:, planes, :], ALU.add)
            nc.sync.dma_start(out_rows[:, planes, :], result[:, planes, :])
